import numpy as np
import ml_dtypes


def mxq(x, axis, fmt="e4m3"):
    dtype, down = {"e4m3": (ml_dtypes.float8_e4m3fn, 7), "e5m2": (ml_dtypes.float8_e5m2, 14)}[fmt]
    v = np.moveaxis(np.asarray(x, np.float32).astype(ml_dtypes.bfloat16).astype(np.float64), axis, -1)
    blocks = v.reshape(v.shape[:-1] + (-1, 32))
    amax = np.abs(blocks).max(-1, keepdims=True)
    byte = np.maximum(np.where(amax > 0, np.frexp(amax)[1] - 1 + 127, 0) - down, 1)
    scale = np.exp2(byte - 127.0)
    codes = (blocks / scale).astype(np.float32).astype(dtype).astype(np.float64)
    return np.moveaxis((codes * scale).reshape(v.shape), -1, axis)


WIDE = False


def mx_kscale(k):
    if not WIDE:
        return np.ones(k)
    levels = np.array([10, -10, 5, -5, 0])
    if k % 512:
        return np.exp2(np.random.permutation(np.resize(levels, k // 32))).repeat(32)
    a = np.empty((k // 512, 16))
    for p in range(k // 512):
        a[p, :8] = np.random.permutation(np.resize(levels, 8))
        for g in range(8):
            far = levels[np.abs(levels - a[p, g]) >= 10]
            a[p, g + 8] = far[np.random.randint(len(far))]
    return np.exp2(a.ravel()).repeat(32)


def f64(x):
    return np.asarray(x).astype(np.float64)


def striped(idx):
    return np.tile(idx.reshape(-1, 16).T, (8, 1)).astype(np.uint16)


def unstriped(offs):
    return offs[:16].T.reshape(-1).astype(np.int64)


def striped8(idx):
    return np.concatenate([x.reshape(-1, 16).T for x in idx]).astype(np.uint16)


def runs(offs, k):
    lists = np.stack([offs[16 * r : 16 * r + 16].T.reshape(-1) for r in range(8)]).astype(np.int64)
    return lists[np.arange(k) % 512 // 64]


def pack_weight(w):
    k, n = w.shape
    w = f64(np.asarray(w, np.float32).astype(ml_dtypes.bfloat16)).reshape(k // 32, 32, n)
    amax = np.abs(w).max(1)
    byte = np.clip(np.where(amax > 0, np.frexp(amax)[1] - 1 + 127 - 7, 1), 1, 254)
    scaled = (w * np.exp2(127.0 - byte)[:, None, :]).reshape(k, n).astype(np.float32)
    words = np.ascontiguousarray(scaled.reshape(k // 512, 128, 4, n).transpose(0, 1, 3, 2)).astype(ml_dtypes.float8_e4m3fn).view(np.uint8)
    return words, np.ascontiguousarray(byte.astype(np.uint8).reshape(k // 512, 16, n))


def unpack_weight(words, scales):
    g, p, n, _ = words.shape
    vals = np.ascontiguousarray(words).view(ml_dtypes.float8_e4m3fn).astype(np.float64) * np.repeat(np.exp2(scales.astype(np.float64) - 127.0), 8, axis=1)[..., None]
    return vals.transpose(0, 1, 3, 2).reshape(g * 512, n)


K, T, S, N, U, H = 512, 2048, 512, 512, 1024, 512


def setup_inputs():
    n = np.random.standard_normal
    s = mx_kscale(K)[:, None]
    u = mx_kscale(H)
    packed_xT = pack_weight(n((K, T)) * s)
    return {
        "x_words": packed_xT[0],
        "x_scales": packed_xT[1],
        "w1": (n((K, H)) / np.sqrt(K) / s * u).astype(np.float32),
        "mem": (n((H, U)) * u[:, None]).astype(np.float32),
        "w2": (n((H, N)) / np.sqrt(H) / u[:, None]).astype(np.float32),
        "offs": striped(np.random.permutation(T)[:S]),
        "slot": striped8(np.stack([np.random.permutation(U)[:S] for _ in range(8)])),
    }


def reference(x_words, x_scales, w1, mem, w2, offs, slot):
    xq = unpack_weight(x_words, x_scales)[:, unstriped(offs)]
    y = mxq(f64(w1), 0, "e4m3").T @ xq
    nw = np.maximum(y, 0.75 * (f64(mem)[np.arange(H)[:, None], runs(slot, H)]))
    dm = 0.75 * f64(mem)
    z = dm.copy()
    z[np.arange(H)[:, None], runs(slot, H)] = nw
    return mxq(f64(w2), 0, "e4m3").T @ mxq(z, 0, "e4m3")

@@ -1,0 +1,133 @@
+from contextlib import ExitStack
+
+import concourse.mybir as mybir
+
+K, T, S, N, U, H = 512, 2048, 512, 512, 1024, 512
+FLOPS = 2 * K * H * S + 2 * H * N * U
+
+F32 = mybir.dt.float32
+BF16 = mybir.dt.bfloat16
+I32 = mybir.dt.int32
+U32 = mybir.dt.uint32
+U16 = mybir.dt.uint16
+U8 = mybir.dt.uint8
+FP8X4 = mybir.dt.float8_e4m3fn_x4
+MULT = mybir.AluOpType.mult
+MAX = mybir.AluOpType.max
+COPY = mybir.ActivationFunctionType.Copy
+
+P = 128
+PACK = 4
+BANK = 512
+DECAY = 0.75
+PLANE_ORDER = (1, 2, 3, 0)
+CHUNKS = (128, 128, 256, 256, 256)
+W1_SPLIT = 80
+VECTOR_BANKS = (5, 7)
+
+
+def tile_picked_decaypage_none_p_kernel(tc, x_words, x_scales, w1, mem, w2, offs, slot, out):
+    nc = tc.nc
+    with ExitStack() as ctx:
+        lists = ctx.enter_context(tc.tile_pool(name="lists", bufs=1))
+        keep = ctx.enter_context(tc.tile_pool(name="keep", bufs=1))
+        shared = ctx.enter_context(tc.tile_pool(name="shared", bufs=1))
+        psum = ctx.enter_context(tc.psum_pool(name="psum", bufs=8))
+
+        offs_sb = lists.tile([P, S // 16], U16, name="offs_sb")
+        slot_sb = lists.tile([P, S // 16], U16, name="slot_sb")
+        xs_all = keep.tile([P, T], U8, name="xs_all", align_bytes=64)
+        nc.vector.memset(xs_all[:].bitcast(I32), 0)
+
+        mem_rows = mem.rearrange("(p t) w -> t p w", t=PACK)
+        mem_sb = {t: keep.tile([P, U], F32, name="mem%d" % t) for t in PLANE_ORDER}
+        w1_raw = keep.tile([P, PACK * H], F32, name="w1_raw")
+        xw_all = keep.tile([P, T], I32, name="xw_all", align_bytes=64)
+        w2_raw = shared.tile([P, PACK * N], F32, name="w2_raw", align_bytes=64, offset=0)
+
+        nc.sync.dma_start(offs_sb[:], offs)
+        nc.sync.dma_start(slot_sb[:], slot)
+        nc.sync.dma_start(mem_sb[PLANE_ORDER[0]][:], mem_rows[PLANE_ORDER[0]])
+        for q in range(4):
+            nc.sync.dma_start(xs_all[32 * q : 32 * q + 4, :].bitcast(I32), x_scales[0, 4 * q : 4 * q + 4, :].bitcast(I32))
+        nc.sync.dma_start(w1_raw[:], w1.rearrange("(p j) c -> p (j c)", j=PACK))
+        nc.sync.dma_start(xw_all[:], x_words[0].rearrange("p n t -> p (n t)").bitcast(I32))
+        for t in PLANE_ORDER[1:]:
+            nc.sync.dma_start(mem_sb[t][:], mem_rows[t])
+        nc.sync.dma_start(w2_raw[:], w2.rearrange("(p j) m -> p (j m)", j=PACK))
+
+        xs = keep.tile([P, S], U8, name="xs", align_bytes=64)
+        nc.vector.tensor_copy(xs[:], xs_all[:].indirect(offs_sb[:]))
+
+        w1_bf = keep.tile([P, PACK * H], BF16, name="w1_bf", align_bytes=64)
+        w1_src = w1_raw[:].rearrange("p (j m t) -> p m j t", j=PACK, t=PACK)
+        w1_dst = w1_bf[:].rearrange("p (t m j) -> p m j t", t=PACK, j=PACK)
+        nc.vector.tensor_copy(w1_dst[:, 0:W1_SPLIT], w1_src[:, 0:W1_SPLIT])
+        nc.scalar.copy(w1_dst[:, W1_SPLIT:P], w1_src[:, W1_SPLIT:P])
+        w1_q = keep.tile([P, H], U32, name="w1_q", align_bytes=64)
+        w1_s = keep.tile([P, H], U8, name="w1_s", align_bytes=64)
+        nc.vector.quantize_mx(w1_q[:].bitcast(FP8X4), w1_s[:], w1_bf[:])
+
+        xw = keep.tile([P, S], U32, name="xw", align_bytes=64)
+        nc.vector.tensor_copy(xw[:], xw_all[:].bitcast(U32).indirect(offs_sb[:]))
+
+        y = {}
+        for t in PLANE_ORDER:
+            y[t] = psum.tile([P, S], F32, name="y%d" % t, tag="bank")
+            cols = slice(P * t, P * (t + 1))
+            nc.tensor.matmul_mx(y[t][:], lhsT=w1_q[:, cols].bitcast(FP8X4), lhsT_scale=w1_s[:, cols],
+                                rhs=xw[:].bitcast(FP8X4), rhs_scale=xs[:], start=True, stop=True)
+
+        z = {t: keep.tile([P, 2 * U if t == 0 else U], F32, name="z%d" % t) for t in PLANE_ORDER}
+        for t in PLANE_ORDER:
+            nc.scalar.activation(z[t][:, 0:U], mem_sb[t][:], COPY, scale=DECAY)
+        w2_bf = keep.tile([P, PACK * N], BF16, name="w2_bf", tag="w2_then_new", align_bytes=64)
+        nc.scalar.copy(w2_bf[:].rearrange("p (c i j) -> p c j i", i=4, j=PACK),
+                       w2_raw[:].rearrange("p (j c i) -> p c j i", j=PACK, i=4))
+        w2_q = keep.tile([P, N], U32, name="w2_q", align_bytes=64)
+        w2_s = keep.tile([P, N], U8, name="w2_s", align_bytes=64)
+        nc.vector.quantize_mx(w2_q[:].bitcast(FP8X4), w2_s[:], w2_bf[:])
+
+        starts = [sum(CHUNKS[:c]) for c in range(len(CHUNKS))]
+        z_bf = [shared.tile([P, PACK * width], BF16, name="z_bf%d" % c, align_bytes=64, offset=2 * PACK * starts[c])
+                for c, width in enumerate(CHUNKS)]
+        z_words = [tile[:].rearrange("p (w j) -> p w j", j=PACK) for tile in z_bf]
+
+        for t in PLANE_ORDER:
+            old = keep.tile([P, S], F32, name="old%d" % t)
+            nc.vector.tensor_copy(old[:], mem_sb[t][:].indirect(slot_sb[:]))
+            if t == 0:
+                new = keep.tile([P, S], F32, name="new0", tag="w2_then_new", align_bytes=64)
+            else:
+                new = keep.tile([P, S], F32, name="new%d" % t)
+            nc.vector.scalar_tensor_tensor(new[:], old[:], DECAY, y[t][:], MULT, MAX)
+            nc.vector.tensor_copy(z[t][:].indirect(slot_sb[:]), new[:])
+            if t == 1:
+                nc.scalar.copy(z[0][:, U : 2 * U], z[1][:])
+            elif t != 0:
+                for c, width in enumerate(CHUNKS):
+                    nc.scalar.copy(z_words[c][:, :, t], z[t][:, starts[c] : starts[c] + width])
+
+        pair = z[0][:].rearrange("p (h w) -> p w h", h=2)
+        out_rows = out.rearrange("(a p) w -> p a w", p=P)
+        bank_no = 0
+        for c, width in enumerate(CHUNKS):
+            cols = slice(starts[c], starts[c] + width)
+            nc.vector.tensor_copy(z_words[c][:, :, 0:2], pair[:, cols, :])
+            z_q = keep.tile([P, width], U32, name="z_q%d" % c, align_bytes=64)
+            z_s = keep.tile([P, width], U8, name="z_s%d" % c, align_bytes=64)
+            nc.vector.quantize_mx(z_q[:].bitcast(FP8X4), z_s[:], z_bf[c][:])
+            per_bank = BANK // width
+            for a0 in range(0, N // P, per_bank):
+                acc = psum.tile([P, per_bank, width], F32, name="acc%d" % bank_no, tag="bank")
+                for a in range(per_bank):
+                    rows = slice(P * (a0 + a), P * (a0 + a + 1))
+                    nc.tensor.matmul_mx(acc[:, a, :], lhsT=w2_q[:, rows].bitcast(FP8X4), lhsT_scale=w2_s[:, rows],
+                                        rhs=z_q[:].bitcast(FP8X4), rhs_scale=z_s[:], start=True, stop=True)
+                res = keep.tile([P, per_bank, width], F32, name="res%d" % bank_no)
+                if bank_no in VECTOR_BANKS:
+                    nc.vector.tensor_copy(res[:], acc[:])
+                else:
+                    nc.scalar.copy(res[:], acc[:])
+                nc.sync.dma_start(out_rows[:, a0 : a0 + per_bank, cols], res[:])
+                bank_no += 1

@@ -21,9 +21,9 @@ PACK = 4
 BANK = 512
 DECAY = 0.75
 PLANE_ORDER = (1, 2, 3, 0)
-CHUNKS = (128, 128, 256, 256, 256)
-W1_SPLIT = 80
-VECTOR_BANKS = (5, 7)
+CHUNKS = (256, 256, 512)
+W1_SPLIT = 72
+VECTOR_BANKS = (3, 5, 7)
 
 
 def tile_picked_decaypage_none_p_kernel(tc, x_words, x_scales, w1, mem, w2, offs, slot, out):
@@ -45,11 +45,11 @@ def tile_picked_decaypage_none_p_kernel(tc, x_words, x_scales, w1, mem, w2, offs
         xw_all = keep.tile([P, T], I32, name="xw_all", align_bytes=64)
         w2_raw = shared.tile([P, PACK * N], F32, name="w2_raw", align_bytes=64, offset=0)
 
-        nc.sync.dma_start(offs_sb[:], offs)
-        nc.sync.dma_start(slot_sb[:], slot)
         nc.sync.dma_start(mem_sb[PLANE_ORDER[0]][:], mem_rows[PLANE_ORDER[0]])
+        nc.sync.dma_start(slot_sb[:], slot)
+        nc.sync.dma_start(offs_sb[:], offs)
         for q in range(4):
-            nc.sync.dma_start(xs_all[32 * q : 32 * q + 4, :].bitcast(I32), x_scales[0, 4 * q : 4 * q + 4, :].bitcast(I32))
+            nc.sync.dma_start(xs_all[q:P:32, :].bitcast(I32), x_scales[0, q:16:4, :].bitcast(I32))
         nc.sync.dma_start(w1_raw[:], w1.rearrange("(p j) c -> p (j c)", j=PACK))
         nc.sync.dma_start(xw_all[:], x_words[0].rearrange("p n t -> p (n t)").bitcast(I32))
         for t in PLANE_ORDER[1:]:
@@ -81,15 +81,12 @@ def tile_picked_decaypage_none_p_kernel(tc, x_words, x_scales, w1, mem, w2, offs
         z = {t: keep.tile([P, 2 * U if t == 0 else U], F32, name="z%d" % t) for t in PLANE_ORDER}
         for t in PLANE_ORDER:
             nc.scalar.activation(z[t][:, 0:U], mem_sb[t][:], COPY, scale=DECAY)
-        w2_bf = keep.tile([P, PACK * N], BF16, name="w2_bf", tag="w2_then_new", align_bytes=64)
+        w2_bf = keep.tile([P, PACK * N], BF16, name="w2_bf", align_bytes=64)
         nc.scalar.copy(w2_bf[:].rearrange("p (c i j) -> p c j i", i=4, j=PACK),
                        w2_raw[:].rearrange("p (j c i) -> p c j i", j=PACK, i=4))
-        w2_q = keep.tile([P, N], U32, name="w2_q", align_bytes=64)
-        w2_s = keep.tile([P, N], U8, name="w2_s", align_bytes=64)
-        nc.vector.quantize_mx(w2_q[:].bitcast(FP8X4), w2_s[:], w2_bf[:])
 
         starts = [sum(CHUNKS[:c]) for c in range(len(CHUNKS))]
-        z_bf = [shared.tile([P, PACK * width], BF16, name="z_bf%d" % c, align_bytes=64, offset=2 * PACK * starts[c])
+        z_bf = [shared.tile([P, PACK * width], BF16, name="z_bf%d" % c, align_bytes=64, offset=4 * S + 2 * PACK * starts[c])
                 for c, width in enumerate(CHUNKS)]
         z_words = [tile[:].rearrange("p (w j) -> p w j", j=PACK) for tile in z_bf]
 
@@ -97,7 +94,7 @@ def tile_picked_decaypage_none_p_kernel(tc, x_words, x_scales, w1, mem, w2, offs
             old = keep.tile([P, S], F32, name="old%d" % t)
             nc.vector.tensor_copy(old[:], mem_sb[t][:].indirect(slot_sb[:]))
             if t == 0:
-                new = keep.tile([P, S], F32, name="new0", tag="w2_then_new", align_bytes=64)
+                new = shared.tile([P, S], F32, name="new0", align_bytes=64, offset=0)
             else:
                 new = keep.tile([P, S], F32, name="new%d" % t)
             nc.vector.scalar_tensor_tensor(new[:], old[:], DECAY, y[t][:], MULT, MAX)
@@ -109,20 +106,30 @@ def tile_picked_decaypage_none_p_kernel(tc, x_words, x_scales, w1, mem, w2, offs
                     nc.scalar.copy(z_words[c][:, :, t], z[t][:, starts[c] : starts[c] + width])
 
         pair = z[0][:].rearrange("p (h w) -> p w h", h=2)
+        nc.scalar.copy(z_words[-1][:, :, 0:2], pair[:, starts[-1] : U, :])
         out_rows = out.rearrange("(a p) w -> p a w", p=P)
         bank_no = 0
+        half = N // 2
+        w2_q = [shared.tile([P, half], U32, name="w2_q%d" % h, align_bytes=64, offset=4 * half * h) for h in range(2)]
+        w2_s = [keep.tile([P, half], U8, name="w2_s%d" % h, align_bytes=64) for h in range(2)]
         for c, width in enumerate(CHUNKS):
             cols = slice(starts[c], starts[c] + width)
-            nc.vector.tensor_copy(z_words[c][:, :, 0:2], pair[:, cols, :])
+            if c < len(CHUNKS) - 1:
+                nc.vector.tensor_copy(z_words[c][:, :, 0:2], pair[:, cols, :])
+            if c == 0:
+                nc.vector.quantize_mx(w2_q[0][:].bitcast(FP8X4), w2_s[0][:], w2_bf[:, 0 : PACK * half])
             z_q = keep.tile([P, width], U32, name="z_q%d" % c, align_bytes=64)
             z_s = keep.tile([P, width], U8, name="z_s%d" % c, align_bytes=64)
             nc.vector.quantize_mx(z_q[:].bitcast(FP8X4), z_s[:], z_bf[c][:])
-            per_bank = BANK // width
-            for a0 in range(0, N // P, per_bank):
+            if c == 0:
+                nc.vector.quantize_mx(w2_q[1][:].bitcast(FP8X4), w2_s[1][:], w2_bf[:, PACK * half : PACK * N])
+            groups = [(0, 1), (1, 1), (2, 2)] if c == 0 else [(a0, BANK // width) for a0 in range(0, N // P, BANK // width)]
+            for a0, per_bank in groups:
                 acc = psum.tile([P, per_bank, width], F32, name="acc%d" % bank_no, tag="bank")
                 for a in range(per_bank):
-                    rows = slice(P * (a0 + a), P * (a0 + a + 1))
-                    nc.tensor.matmul_mx(acc[:, a, :], lhsT=w2_q[:, rows].bitcast(FP8X4), lhsT_scale=w2_s[:, rows],
+                    h, first = divmod(P * (a0 + a), half)
+                    rows = slice(first, first + P)
+                    nc.tensor.matmul_mx(acc[:, a, :], lhsT=w2_q[h][:, rows].bitcast(FP8X4), lhsT_scale=w2_s[h][:, rows],
                                         rhs=z_q[:].bitcast(FP8X4), rhs_scale=z_s[:], start=True, stop=True)
                 res = keep.tile([P, per_bank, width], F32, name="res%d" % bank_no)
                 if bank_no in VECTOR_BANKS:

@@ -19,11 +19,14 @@ COPY = mybir.ActivationFunctionType.Copy
 P = 128
 PACK = 4
 BANK = 512
+QUADRANT = 32
 DECAY = 0.75
-PLANE_ORDER = (1, 2, 3, 0)
+
+PLANE_ORDER = (2, 1, 3, 0)
 CHUNKS = (256, 256, 512)
+FIRST_CHUNK_BANKS = [(0, 1), (1, 1), (2, 2)]
 W1_SPLIT = 72
-VECTOR_BANKS = (3, 5, 7)
+VECTOR_BANKS = (5, 6, 8)
 
 
 def tile_picked_decaypage_none_p_kernel(tc, x_words, x_scales, w1, mem, w2, offs, slot, out):
@@ -31,7 +34,8 @@ def tile_picked_decaypage_none_p_kernel(tc, x_words, x_scales, w1, mem, w2, offs
     with ExitStack() as ctx:
         lists = ctx.enter_context(tc.tile_pool(name="lists", bufs=1))
         keep = ctx.enter_context(tc.tile_pool(name="keep", bufs=1))
-        shared = ctx.enter_context(tc.tile_pool(name="shared", bufs=1))
+        after_w2 = ctx.enter_context(tc.tile_pool(name="after_w2", bufs=1))
+        after_mem3 = ctx.enter_context(tc.tile_pool(name="after_mem3", bufs=1))
         psum = ctx.enter_context(tc.psum_pool(name="psum", bufs=8))
 
         offs_sb = lists.tile([P, S // 16], U16, name="offs_sb")
@@ -40,16 +44,17 @@ def tile_picked_decaypage_none_p_kernel(tc, x_words, x_scales, w1, mem, w2, offs
         nc.vector.memset(xs_all[:].bitcast(I32), 0)
 
         mem_rows = mem.rearrange("(p t) w -> t p w", t=PACK)
-        mem_sb = {t: keep.tile([P, U], F32, name="mem%d" % t) for t in PLANE_ORDER}
+        mem_sb = {t: keep.tile([P, U], F32, name="mem%d" % t) for t in PLANE_ORDER if t != 3}
+        mem_sb[3] = after_mem3.tile([P, U], F32, name="mem3", offset=0)
         w1_raw = keep.tile([P, PACK * H], F32, name="w1_raw")
         xw_all = keep.tile([P, T], I32, name="xw_all", align_bytes=64)
-        w2_raw = shared.tile([P, PACK * N], F32, name="w2_raw", align_bytes=64, offset=0)
+        w2_raw = after_w2.tile([P, PACK * N], F32, name="w2_raw", align_bytes=64, offset=0)
 
         nc.sync.dma_start(mem_sb[PLANE_ORDER[0]][:], mem_rows[PLANE_ORDER[0]])
         nc.sync.dma_start(slot_sb[:], slot)
         nc.sync.dma_start(offs_sb[:], offs)
-        for q in range(4):
-            nc.sync.dma_start(xs_all[q:P:32, :].bitcast(I32), x_scales[0, q:16:4, :].bitcast(I32))
+        for r in range(4):
+            nc.sync.dma_start(xs_all[r:P:QUADRANT, :].bitcast(I32), x_scales[0, r:16:4, :].bitcast(I32))
         nc.sync.dma_start(w1_raw[:], w1.rearrange("(p j) c -> p (j c)", j=PACK))
         nc.sync.dma_start(xw_all[:], x_words[0].rearrange("p n t -> p (n t)").bitcast(I32))
         for t in PLANE_ORDER[1:]:
@@ -74,8 +79,8 @@ def tile_picked_decaypage_none_p_kernel(tc, x_words, x_scales, w1, mem, w2, offs
         y = {}
         for t in PLANE_ORDER:
             y[t] = psum.tile([P, S], F32, name="y%d" % t, tag="bank")
-            cols = slice(P * t, P * (t + 1))
-            nc.tensor.matmul_mx(y[t][:], lhsT=w1_q[:, cols].bitcast(FP8X4), lhsT_scale=w1_s[:, cols],
+            w1_cols = slice(P * t, P * (t + 1))
+            nc.tensor.matmul_mx(y[t][:], lhsT=w1_q[:, w1_cols].bitcast(FP8X4), lhsT_scale=w1_s[:, w1_cols],
                                 rhs=xw[:].bitcast(FP8X4), rhs_scale=xs[:], start=True, stop=True)
 
         z = {t: keep.tile([P, 2 * U if t == 0 else U], F32, name="z%d" % t) for t in PLANE_ORDER}
@@ -86,36 +91,46 @@ def tile_picked_decaypage_none_p_kernel(tc, x_words, x_scales, w1, mem, w2, offs
                        w2_raw[:].rearrange("p (j c i) -> p c j i", j=PACK, i=4))
 
         starts = [sum(CHUNKS[:c]) for c in range(len(CHUNKS))]
-        z_bf = [shared.tile([P, PACK * width], BF16, name="z_bf%d" % c, align_bytes=64, offset=4 * S + 2 * PACK * starts[c])
+        z_bf = [after_w2.tile([P, PACK * width], BF16, name="z_bf%d" % c, align_bytes=64, offset=4 * S + 2 * PACK * starts[c])
                 for c, width in enumerate(CHUNKS)]
-        z_words = [tile[:].rearrange("p (w j) -> p w j", j=PACK) for tile in z_bf]
+        z_cols = [tile[:].rearrange("p (w j) -> p w j", j=PACK) for tile in z_bf]
 
+        old = {t: keep.tile([P, S], F32, name="old%d" % t, tag="old%d" % t) for t in PLANE_ORDER}
         for t in PLANE_ORDER:
-            old = keep.tile([P, S], F32, name="old%d" % t)
-            nc.vector.tensor_copy(old[:], mem_sb[t][:].indirect(slot_sb[:]))
+            nc.vector.tensor_copy(old[t][:], mem_sb[t][:].indirect(slot_sb[:]))
+        new = {}
+
+        def raise_plane(t):
             if t == 0:
-                new = shared.tile([P, S], F32, name="new0", align_bytes=64, offset=0)
+                new[t] = after_w2.tile([P, S], F32, name="new0", align_bytes=64, offset=0)
+            elif t == 3:
+                new[t] = keep.tile([P, S], F32, name="new3", tag="old2")
             else:
-                new = keep.tile([P, S], F32, name="new%d" % t)
-            nc.vector.scalar_tensor_tensor(new[:], old[:], DECAY, y[t][:], MULT, MAX)
-            nc.vector.tensor_copy(z[t][:].indirect(slot_sb[:]), new[:])
+                new[t] = after_mem3.tile([P, S], F32, name="new%d" % t, offset=4 * S * (t - 1))
+            nc.vector.scalar_tensor_tensor(new[t][:], old[t][:], DECAY, y[t][:], MULT, MAX)
+
+        raise_plane(PLANE_ORDER[0])
+        for step, t in enumerate(PLANE_ORDER):
+            if step + 1 < PACK:
+                raise_plane(PLANE_ORDER[step + 1])
+            nc.vector.tensor_copy(z[t][:].indirect(slot_sb[:]), new[t][:])
             if t == 1:
                 nc.scalar.copy(z[0][:, U : 2 * U], z[1][:])
             elif t != 0:
                 for c, width in enumerate(CHUNKS):
-                    nc.scalar.copy(z_words[c][:, :, t], z[t][:, starts[c] : starts[c] + width])
+                    nc.scalar.copy(z_cols[c][:, :, t], z[t][:, starts[c] : starts[c] + width])
 
         pair = z[0][:].rearrange("p (h w) -> p w h", h=2)
-        nc.scalar.copy(z_words[-1][:, :, 0:2], pair[:, starts[-1] : U, :])
+        nc.scalar.copy(z_cols[-1][:, :, 0:2], pair[:, starts[-1] : U, :])
         out_rows = out.rearrange("(a p) w -> p a w", p=P)
         bank_no = 0
         half = N // 2
-        w2_q = [shared.tile([P, half], U32, name="w2_q%d" % h, align_bytes=64, offset=4 * half * h) for h in range(2)]
+        w2_q = [after_w2.tile([P, half], U32, name="w2_q%d" % h, align_bytes=64, offset=4 * half * h) for h in range(2)]
         w2_s = [keep.tile([P, half], U8, name="w2_s%d" % h, align_bytes=64) for h in range(2)]
         for c, width in enumerate(CHUNKS):
             cols = slice(starts[c], starts[c] + width)
             if c < len(CHUNKS) - 1:
-                nc.vector.tensor_copy(z_words[c][:, :, 0:2], pair[:, cols, :])
+                nc.vector.tensor_copy(z_cols[c][:, :, 0:2], pair[:, cols, :])
             if c == 0:
                 nc.vector.quantize_mx(w2_q[0][:].bitcast(FP8X4), w2_s[0][:], w2_bf[:, 0 : PACK * half])
             z_q = keep.tile([P, width], U32, name="z_q%d" % c, align_bytes=64)
@@ -123,13 +138,13 @@ def tile_picked_decaypage_none_p_kernel(tc, x_words, x_scales, w1, mem, w2, offs
             nc.vector.quantize_mx(z_q[:].bitcast(FP8X4), z_s[:], z_bf[c][:])
             if c == 0:
                 nc.vector.quantize_mx(w2_q[1][:].bitcast(FP8X4), w2_s[1][:], w2_bf[:, PACK * half : PACK * N])
-            groups = [(0, 1), (1, 1), (2, 2)] if c == 0 else [(a0, BANK // width) for a0 in range(0, N // P, BANK // width)]
-            for a0, per_bank in groups:
+            banks = FIRST_CHUNK_BANKS if c == 0 else [(a0, BANK // width) for a0 in range(0, N // P, BANK // width)]
+            for a0, per_bank in banks:
                 acc = psum.tile([P, per_bank, width], F32, name="acc%d" % bank_no, tag="bank")
                 for a in range(per_bank):
                     h, first = divmod(P * (a0 + a), half)
-                    rows = slice(first, first + P)
-                    nc.tensor.matmul_mx(acc[:, a, :], lhsT=w2_q[h][:, rows].bitcast(FP8X4), lhsT_scale=w2_s[h][:, rows],
+                    w2_cols = slice(first, first + P)
+                    nc.tensor.matmul_mx(acc[:, a, :], lhsT=w2_q[h][:, w2_cols].bitcast(FP8X4), lhsT_scale=w2_s[h][:, w2_cols],
                                         rhs=z_q[:].bitcast(FP8X4), rhs_scale=z_s[:], start=True, stop=True)
                 res = keep.tile([P, per_bank, width], F32, name="res%d" % bank_no)
                 if bank_no in VECTOR_BANKS:

from contextlib import ExitStack

import concourse.mybir as mybir

K, T, S, N, U, H = 512, 2048, 512, 512, 1024, 512
FLOPS = 2 * K * H * S + 2 * H * N * U

F32 = mybir.dt.float32
BF16 = mybir.dt.bfloat16
I32 = mybir.dt.int32
U32 = mybir.dt.uint32
U16 = mybir.dt.uint16
U8 = mybir.dt.uint8
FP8X4 = mybir.dt.float8_e4m3fn_x4
MULT = mybir.AluOpType.mult
MAX = mybir.AluOpType.max
COPY = mybir.ActivationFunctionType.Copy

P = 128
PACK = 4
BANK = 512
QUADRANT = 32
DECAY = 0.75

PLANE_ORDER = (2, 1, 3, 0)
CHUNKS = (256, 256, 512)
FIRST_CHUNK_BANKS = [(0, 1), (1, 1), (2, 2)]
W1_SPLIT = 72
VECTOR_BANKS = (5, 6, 8)


def tile_picked_decaypage_none_p_kernel(tc, x_words, x_scales, w1, mem, w2, offs, slot, out):
    nc = tc.nc
    with ExitStack() as ctx:
        lists = ctx.enter_context(tc.tile_pool(name="lists", bufs=1))
        keep = ctx.enter_context(tc.tile_pool(name="keep", bufs=1))
        after_w2 = ctx.enter_context(tc.tile_pool(name="after_w2", bufs=1))
        after_mem3 = ctx.enter_context(tc.tile_pool(name="after_mem3", bufs=1))
        psum = ctx.enter_context(tc.psum_pool(name="psum", bufs=8))

        offs_sb = lists.tile([P, S // 16], U16, name="offs_sb")
        slot_sb = lists.tile([P, S // 16], U16, name="slot_sb")
        xs_all = keep.tile([P, T], U8, name="xs_all", align_bytes=64)
        nc.vector.memset(xs_all[:].bitcast(I32), 0)

        mem_rows = mem.rearrange("(p t) w -> t p w", t=PACK)
        mem_sb = {t: keep.tile([P, U], F32, name="mem%d" % t) for t in PLANE_ORDER if t != 3}
        mem_sb[3] = after_mem3.tile([P, U], F32, name="mem3", offset=0)
        w1_raw = keep.tile([P, PACK * H], F32, name="w1_raw")
        xw_all = keep.tile([P, T], I32, name="xw_all", align_bytes=64)
        w2_raw = after_w2.tile([P, PACK * N], F32, name="w2_raw", align_bytes=64, offset=0)

        nc.sync.dma_start(mem_sb[PLANE_ORDER[0]][:], mem_rows[PLANE_ORDER[0]])
        nc.sync.dma_start(slot_sb[:], slot)
        nc.sync.dma_start(offs_sb[:], offs)
        for r in range(4):
            nc.sync.dma_start(xs_all[r:P:QUADRANT, :].bitcast(I32), x_scales[0, r:16:4, :].bitcast(I32))
        nc.sync.dma_start(w1_raw[:], w1.rearrange("(p j) c -> p (j c)", j=PACK))
        nc.sync.dma_start(xw_all[:], x_words[0].rearrange("p n t -> p (n t)").bitcast(I32))
        for t in PLANE_ORDER[1:]:
            nc.sync.dma_start(mem_sb[t][:], mem_rows[t])
        nc.sync.dma_start(w2_raw[:], w2.rearrange("(p j) m -> p (j m)", j=PACK))

        xs = keep.tile([P, S], U8, name="xs", align_bytes=64)
        nc.vector.tensor_copy(xs[:], xs_all[:].indirect(offs_sb[:]))

        w1_bf = keep.tile([P, PACK * H], BF16, name="w1_bf", align_bytes=64)
        w1_src = w1_raw[:].rearrange("p (j m t) -> p m j t", j=PACK, t=PACK)
        w1_dst = w1_bf[:].rearrange("p (t m j) -> p m j t", t=PACK, j=PACK)
        nc.vector.tensor_copy(w1_dst[:, 0:W1_SPLIT], w1_src[:, 0:W1_SPLIT])
        nc.scalar.copy(w1_dst[:, W1_SPLIT:P], w1_src[:, W1_SPLIT:P])
        w1_q = keep.tile([P, H], U32, name="w1_q", align_bytes=64)
        w1_s = keep.tile([P, H], U8, name="w1_s", align_bytes=64)
        nc.vector.quantize_mx(w1_q[:].bitcast(FP8X4), w1_s[:], w1_bf[:])

        xw = keep.tile([P, S], U32, name="xw", align_bytes=64)
        nc.vector.tensor_copy(xw[:], xw_all[:].bitcast(U32).indirect(offs_sb[:]))

        y = {}
        for t in PLANE_ORDER:
            y[t] = psum.tile([P, S], F32, name="y%d" % t, tag="bank")
            w1_cols = slice(P * t, P * (t + 1))
            nc.tensor.matmul_mx(y[t][:], lhsT=w1_q[:, w1_cols].bitcast(FP8X4), lhsT_scale=w1_s[:, w1_cols],
                                rhs=xw[:].bitcast(FP8X4), rhs_scale=xs[:], start=True, stop=True)

        z = {t: keep.tile([P, 2 * U if t == 0 else U], F32, name="z%d" % t) for t in PLANE_ORDER}
        for t in PLANE_ORDER:
            nc.scalar.activation(z[t][:, 0:U], mem_sb[t][:], COPY, scale=DECAY)
        w2_bf = keep.tile([P, PACK * N], BF16, name="w2_bf", align_bytes=64)
        nc.scalar.copy(w2_bf[:].rearrange("p (c i j) -> p c j i", i=4, j=PACK),
                       w2_raw[:].rearrange("p (j c i) -> p c j i", j=PACK, i=4))

        starts = [sum(CHUNKS[:c]) for c in range(len(CHUNKS))]
        z_bf = [after_w2.tile([P, PACK * width], BF16, name="z_bf%d" % c, align_bytes=64, offset=4 * S + 2 * PACK * starts[c])
                for c, width in enumerate(CHUNKS)]
        z_cols = [tile[:].rearrange("p (w j) -> p w j", j=PACK) for tile in z_bf]

        old = {t: keep.tile([P, S], F32, name="old%d" % t, tag="old%d" % t) for t in PLANE_ORDER}
        for t in PLANE_ORDER:
            nc.vector.tensor_copy(old[t][:], mem_sb[t][:].indirect(slot_sb[:]))
        new = {}

        def raise_plane(t):
            if t == 0:
                new[t] = after_w2.tile([P, S], F32, name="new0", align_bytes=64, offset=0)
            elif t == 3:
                new[t] = keep.tile([P, S], F32, name="new3", tag="old2")
            else:
                new[t] = after_mem3.tile([P, S], F32, name="new%d" % t, offset=4 * S * (t - 1))
            nc.vector.scalar_tensor_tensor(new[t][:], old[t][:], DECAY, y[t][:], MULT, MAX)

        raise_plane(PLANE_ORDER[0])
        for step, t in enumerate(PLANE_ORDER):
            if step + 1 < PACK:
                raise_plane(PLANE_ORDER[step + 1])
            nc.vector.tensor_copy(z[t][:].indirect(slot_sb[:]), new[t][:])
            if t == 1:
                nc.scalar.copy(z[0][:, U : 2 * U], z[1][:])
            elif t != 0:
                for c, width in enumerate(CHUNKS):
                    nc.scalar.copy(z_cols[c][:, :, t], z[t][:, starts[c] : starts[c] + width])

        pair = z[0][:].rearrange("p (h w) -> p w h", h=2)
        nc.scalar.copy(z_cols[-1][:, :, 0:2], pair[:, starts[-1] : U, :])
        out_rows = out.rearrange("(a p) w -> p a w", p=P)
        bank_no = 0
        half = N // 2
        w2_q = [after_w2.tile([P, half], U32, name="w2_q%d" % h, align_bytes=64, offset=4 * half * h) for h in range(2)]
        w2_s = [keep.tile([P, half], U8, name="w2_s%d" % h, align_bytes=64) for h in range(2)]
        for c, width in enumerate(CHUNKS):
            cols = slice(starts[c], starts[c] + width)
            if c < len(CHUNKS) - 1:
                nc.vector.tensor_copy(z_cols[c][:, :, 0:2], pair[:, cols, :])
            if c == 0:
                nc.vector.quantize_mx(w2_q[0][:].bitcast(FP8X4), w2_s[0][:], w2_bf[:, 0 : PACK * half])
            z_q = keep.tile([P, width], U32, name="z_q%d" % c, align_bytes=64)
            z_s = keep.tile([P, width], U8, name="z_s%d" % c, align_bytes=64)
            nc.vector.quantize_mx(z_q[:].bitcast(FP8X4), z_s[:], z_bf[c][:])
            if c == 0:
                nc.vector.quantize_mx(w2_q[1][:].bitcast(FP8X4), w2_s[1][:], w2_bf[:, PACK * half : PACK * N])
            banks = FIRST_CHUNK_BANKS if c == 0 else [(a0, BANK // width) for a0 in range(0, N // P, BANK // width)]
            for a0, per_bank in banks:
                acc = psum.tile([P, per_bank, width], F32, name="acc%d" % bank_no, tag="bank")
                for a in range(per_bank):
                    h, first = divmod(P * (a0 + a), half)
                    w2_cols = slice(first, first + P)
                    nc.tensor.matmul_mx(acc[:, a, :], lhsT=w2_q[h][:, w2_cols].bitcast(FP8X4), lhsT_scale=w2_s[h][:, w2_cols],
                                        rhs=z_q[:].bitcast(FP8X4), rhs_scale=z_s[:], start=True, stop=True)
                res = keep.tile([P, per_bank, width], F32, name="res%d" % bank_no)
                if bank_no in VECTOR_BANKS:
                    nc.vector.tensor_copy(res[:], acc[:])
                else:
                    nc.scalar.copy(res[:], acc[:])
                nc.sync.dma_start(out_rows[:, a0 : a0 + per_bank, cols], res[:])
                bank_no += 1
